import numpy as np
import ml_dtypes


def mxq(x, axis, fmt="e4m3"):
    dtype, down = {"e4m3": (ml_dtypes.float8_e4m3fn, 7), "e5m2": (ml_dtypes.float8_e5m2, 14)}[fmt]
    v = np.moveaxis(np.asarray(x, np.float32).astype(ml_dtypes.bfloat16).astype(np.float64), axis, -1)
    blocks = v.reshape(v.shape[:-1] + (-1, 32))
    amax = np.abs(blocks).max(-1, keepdims=True)
    byte = np.maximum(np.where(amax > 0, np.frexp(amax)[1] - 1 + 127, 0) - down, 1)
    scale = np.exp2(byte - 127.0)
    codes = (blocks / scale).astype(np.float32).astype(dtype).astype(np.float64)
    return np.moveaxis((codes * scale).reshape(v.shape), -1, axis)


WIDE = False


def mx_kscale(k):
    if not WIDE:
        return np.ones(k)
    levels = np.array([10, -10, 5, -5, 0])
    if k % 512:
        return np.exp2(np.random.permutation(np.resize(levels, k // 32))).repeat(32)
    a = np.empty((k // 512, 16))
    for p in range(k // 512):
        a[p, :8] = np.random.permutation(np.resize(levels, 8))
        for g in range(8):
            far = levels[np.abs(levels - a[p, g]) >= 10]
            a[p, g + 8] = far[np.random.randint(len(far))]
    return np.exp2(a.ravel()).repeat(32)


def f64(x):
    return np.asarray(x).astype(np.float64)


def striped(idx):
    return np.tile(np.asarray(idx).reshape(-1, 16).T, (8, 1)).astype(np.uint16)


def unstriped(offs):
    return offs[:16].T.reshape(-1).astype(np.int64)


E2M1 = np.array([0.0, 0.5, 1.0, 1.5, 2.0, 3.0, 4.0, 6.0, -0.0, -0.5, -1.0, -1.5, -2.0, -3.0, -4.0, -6.0])


def pack_weight(w, fmt):
    k, n = w.shape
    w = f64(np.asarray(w, np.float32).astype(ml_dtypes.bfloat16)).reshape(k // 32, 32, n)
    amax = np.abs(w).max(1)
    if fmt == "e4m3":
        byte = np.frexp(amax)[1] - 1 + 127 - 7
    else:
        mant, ex = np.frexp(amax / 6.0)
        byte = np.where(mant > 0.5, ex, ex - 1) + 127
    byte = np.clip(np.where(amax > 0, byte, 1), 1, 254)
    scaled = (w * np.exp2(127.0 - byte)[:, None, :]).reshape(k, n).astype(np.float32)
    by_word = np.ascontiguousarray(scaled.reshape(k // 512, 128, 4, n).transpose(0, 1, 3, 2))
    if fmt == "e4m3":
        words = by_word.astype(ml_dtypes.float8_e4m3fn).view(np.uint8)
    else:
        c = by_word.astype(ml_dtypes.float4_e2m1fn).view(np.uint8) & 0xF
        words = (c[..., 0::2] | (c[..., 1::2] << 4)).reshape(k // 512, 128, 2 * n)
    return np.ascontiguousarray(words), np.ascontiguousarray(byte.astype(np.uint8).reshape(k // 512, 16, n))


def unpack_weight(words, scales, fmt):
    g, _, n = scales.shape
    words = np.ascontiguousarray(words).reshape(g, 128, n, -1)
    if fmt == "e4m3":
        vals = words.view(ml_dtypes.float8_e4m3fn).astype(np.float64)
    else:
        nib = np.empty((g, 128, n, 4), np.uint8)
        nib[..., 0::2] = words & 0xF
        nib[..., 1::2] = words >> 4
        vals = E2M1[nib]
    vals = vals * np.repeat(np.exp2(scales.astype(np.float64) - 127.0), 8, axis=1)[..., None]
    return vals.transpose(0, 1, 3, 2).reshape(g * 512, n)


def sigmoid(v):
    return 1.0 / (1.0 + np.exp(-v))


D, E, T, I, Q, G, B = 512, 512, 2048, 512, 128, 64, 8


def setup_inputs():
    n = np.random.standard_normal
    idx = np.random.permutation(T)[:I]
    fd = mx_kscale(D)
    fe = mx_kscale(E)
    keysp = pack_weight(n((D, T)) / fd[:, None], "e4m3")
    valsp = pack_weight(n((E, T)) / fe[:, None], "e4m3")
    return {
        "query": (n((D, Q)) * 0.8 / np.sqrt(D) * fd[:, None]).astype(np.float32),
        "keys_words": keysp[0],
        "keys_scales": keysp[1],
        "steep": (np.random.uniform(2.0, 8.0, (Q, 1))).astype(np.float32),
        "gout": (n((E, Q)) * 1 / np.sqrt(E) * fe[:, None]).astype(np.float32),
        "vals_words": valsp[0],
        "vals_scales": valsp[1],
        "dquery": (n((D, Q)) * 1.0 / np.sqrt(D) * fd[:, None]).astype(np.float32),
        "base": (0.5 * n((Q, T))).astype(np.float32),
        "offs": striped(idx),
    }


def reference(query, keys_words, keys_scales, steep, gout, vals_words, vals_scales, dquery, base, offs):
    idx = unstriped(offs)
    keysu = unpack_weight(keys_words, keys_scales, "e4m3")
    valsu = unpack_weight(vals_words, vals_scales, "e4m3")
    queryq = mxq(f64(query), 0, "e4m3")
    keysidxg = keysu[:, idx]
    a = queryq.T @ keysidxg
    dqueryq = mxq(f64(dquery), 0, "e4m3")
    ta = dqueryq.T @ keysidxg
    m1 = a.reshape(Q, G, I // G).mean(axis=2)
    m2 = m1.reshape(Q, B, G // B).mean(axis=2)
    mr = np.repeat(m2, G // B, axis=1)
    g1 = sigmoid((m1 - mr) * f64(steep))
    gr = np.repeat(g1, I // G, axis=1)
    p = np.exp(a) * gr
    z = np.sum(p, axis=1, keepdims=True)
    goutq = mxq(f64(gout), 0, "e4m3")
    valsidxg = valsu[:, idx]
    c0 = goutq.T @ valsidxg
    dz = np.sum(c0 * p / np.square(z) * (-1.0), axis=1, keepdims=True)
    dp = c0 / z + dz
    dgr = dp * np.exp(a)
    dg1 = dgr.reshape(Q, G, I // G).sum(axis=2)
    tm1 = ta.reshape(Q, G, I // G).mean(axis=2)
    tm2 = tm1.reshape(Q, B, G // B).mean(axis=2)
    tmr = np.repeat(tm2, G // B, axis=1)
    tg1 = (tm1 - tmr) * f64(steep) * g1 * (1.0 - g1)
    tgr = np.repeat(tg1, I // G, axis=1)
    tp = ta * np.exp(a) * gr + tgr * np.exp(a)
    tz = np.sum(tp, axis=1, keepdims=True)
    tdz = np.sum((tp * c0 - tz * z * 2.0 * c0 * p / np.square(z)) / np.square(z) * (-1.0), axis=1, keepdims=True)
    tdp = tz * c0 / np.square(z) * (-1.0) + tdz
    tdgr = tdp * np.exp(a) + ta * np.exp(a) * dp
    tdg1 = tdgr.reshape(Q, G, I // G).sum(axis=2)
    tdmr = ((tdg1 * g1 + tg1 * dg1) * (1.0 - g1) + tg1 * (-1.0) * dg1 * g1) * f64(steep) * (-1.0)
    tdm2 = tdmr.reshape(Q, B, G // B).sum(axis=2)
    te1 = tdm2 / 8.0
    tr1 = np.repeat(te1, G // B, axis=1)
    tdm1 = ((tdg1 * g1 + tg1 * dg1) * (1.0 - g1) + tg1 * (-1.0) * dg1 * g1) * f64(steep) + tr1
    te2 = tdm1 / 8.0
    tr2 = np.repeat(te2, I // G, axis=1)
    tda = (tdp * gr + tgr * dp) * np.exp(a) + ta * np.exp(a) * dp * gr + tr2
    gs = tda * 512.0
    gf = np.zeros((Q, T))
    gf[:, idx] = gs
    y = f64(base) + gf
    return y

@@ -1,0 +1,247 @@
+import math
+from contextlib import ExitStack
+
+import concourse.mybir as mybir
+
+D, T, I, Q, G, B = 512, 2048, 512, 128, 64, 8
+GROUP = I // G
+FLOPS = 3 * 2 * D * Q * I
+
+F32 = mybir.dt.float32
+BF16 = mybir.dt.bfloat16
+I32 = mybir.dt.int32
+U32 = mybir.dt.uint32
+U16 = mybir.dt.uint16
+U8 = mybir.dt.uint8
+FP8X4 = mybir.dt.float8_e4m3fn_x4
+ALU = mybir.AluOpType
+ACT = mybir.ActivationFunctionType
+AX = mybir.AxisListType
+
+P = 128
+PACK = 4
+SOFT = 8.0
+OUT_CHUNKS = [256, 512, 512, 512, 256]
+
+
+def tile_attend_hvblockcontrast_s_kernel(
+    tc, query, keys_words, keys_scales, steep, gout, vals_words, vals_scales, dquery, base, offs, out
+):
+    nc = tc.nc
+    with ExitStack() as ctx:
+        keep = ctx.enter_context(tc.tile_pool(name="keep", bufs=1))
+        psum = ctx.enter_context(tc.psum_pool(name="psum", bufs=1))
+
+        def tile(name, shape, dtype=F32, tag=None):
+            return keep.tile(shape, dtype, name=name, tag=tag or name, align_bytes=64)
+
+        def by_group(ap):
+            return ap.rearrange("p (g j) -> p g j", j=GROUP)
+
+        def spread(ap):
+            return ap.unsqueeze(2).to_broadcast([P, ap.shape[1], GROUP])
+
+        offsets = keep.tile([P, I // 16], U16, name="offsets")
+        nc.sync.dma_start(offsets[:], offs)
+
+        def load_scales(name, src, engine):
+            plane = tile(name, [P, T], U8)
+            engine.memset(plane[:].bitcast(I32), 0)
+            for quad in range(4):
+                nc.sync.dma_start(
+                    plane[32 * quad : 32 * quad + 4, :].bitcast(I32), src[0, 4 * quad : 4 * quad + 4, :].bitcast(I32)
+                )
+            return plane
+
+        def load_words(name, src):
+            words = tile(name, [P, T], U32)
+            nc.sync.dma_start(words[:].bitcast(I32), src[0].rearrange("p n t -> p (n t)").bitcast(I32))
+            return words
+
+        def load_rows(name, src):
+            raw = tile(name, [P, PACK, Q])
+            nc.sync.dma_start(raw[:], src.rearrange("(p j) w -> p j w", j=PACK))
+            return raw
+
+        def interleave(name, raw):
+            grouped = tile(name, [P, Q, PACK], BF16)
+            nc.scalar.copy(
+                grouped[:].rearrange("p (c i) t -> p c t i", i=4), raw[:].rearrange("p t (c i) -> p c t i", i=4)
+            )
+            return grouped
+
+        def quantize(name, grouped):
+            codes = tile(name + "_codes", [P, Q], U32)
+            scales = tile(name + "_scales", [P, Q], U8)
+            nc.vector.quantize_mx(
+                out=codes[:].bitcast(FP8X4), scales=scales[:], in_=grouped[:].rearrange("p w j -> p (w j)")
+            )
+            return codes, scales
+
+        def gather(name, window, dtype, tag=None):
+            picked = tile(name, [P, I], dtype, tag)
+            nc.vector.tensor_copy(picked[:], window[:].indirect(offsets[:]))
+            return picked
+
+        def product(name, rows, words, scales):
+            bank = psum.tile([P, I], F32, name=name)
+            nc.tensor.matmul_mx(
+                out=bank[:],
+                lhsT=rows[0][:].bitcast(FP8X4),
+                lhsT_scale=rows[1][:],
+                rhs=words[:].bitcast(FP8X4),
+                rhs_scale=scales[:],
+                start=True,
+                stop=True,
+            )
+            return bank
+
+        q_raw = load_rows("q_raw", query)
+        dq_raw = load_rows("dq_raw", dquery)
+        key_plane = load_scales("key_plane", keys_scales, nc.vector)
+        key_pool = load_words("key_pool", keys_words)
+        val_plane = load_scales("val_plane", vals_scales, nc.vector)
+        st = tile("st", [P, 1])
+        nc.sync.dma_start(st[:], steep)
+        go_raw = load_rows("go_raw", gout)
+        val_pool = load_words("val_pool", vals_words)
+        rest = tile("rest", [P, T])
+        nc.sync.dma_start(rest[:], base)
+
+        window = tile("window", [P, T])
+        nc.vector.memset(window[:], 0.0)
+
+        key_scales = gather("key_scales", key_plane, U8)
+        q_bf = interleave("q_bf", q_raw)
+        dq_bf = interleave("dq_bf", dq_raw)
+        q_mx = quantize("q", q_bf)
+        dq_mx = quantize("dq", dq_bf)
+        key_words = gather("key_words", key_pool, U32)
+        val_scales = gather("val_scales", val_plane, U8, "q_bf")
+        a = product("a", q_mx, key_words, key_scales)
+        ta = product("ta", dq_mx, key_words, key_scales)
+
+        sums = tile("sums", [P, 2 * G])
+        nc.vector.tensor_reduce(sums[:, 0:G], by_group(a[:]), AX.X, ALU.add)
+
+        soft = tile("soft", [P, I])
+        soft_sum = tile("soft_sum", [P, 1])
+        shift = tile("shift", [P, 1])
+        e = tile("e", [P, I])
+        nc.scalar.activation(soft[:], a[:], ACT.Exp, scale=1.0 / SOFT, accum_out=soft_sum[:])
+        nc.scalar.activation(
+            shift[:],
+            soft_sum[:].bitcast(U32),
+            ACT.Copy,
+            scale=-SOFT * math.log(2.0) / 2.0**23,
+            bias=SOFT * (127.0 * math.log(2.0) + math.log(I)),
+        )
+        nc.scalar.activation(e[:], a[:], ACT.Exp, bias=shift[:])
+
+        nc.vector.tensor_reduce(sums[:, G : 2 * G], by_group(ta[:]), AX.X, ALU.add)
+        block_a = tile("block_sums", [P, B])
+        block_t = tile("block_t", [P, B])
+        gap = tile("gap", [P, 2 * G])
+        nc.vector.tensor_reduce(block_a[:], by_group(sums[:, 0:G]), AX.X, ALU.add)
+        nc.vector.scalar_tensor_tensor(
+            by_group(gap[:, 0:G]), spread(block_a[:]), 1.0 / 8.0, by_group(sums[:, 0:G]), ALU.mult, ALU.subtract
+        )
+        nc.vector.tensor_reduce(block_t[:], by_group(sums[:, G : 2 * G]), AX.X, ALU.add)
+        nc.vector.scalar_tensor_tensor(
+            by_group(gap[:, G : 2 * G]),
+            spread(block_t[:]),
+            1.0 / 8.0,
+            by_group(sums[:, G : 2 * G]),
+            ALU.mult,
+            ALU.subtract,
+        )
+
+        st_m2 = tile("st_m2", [P, 1])
+        st_m16 = tile("st_m16", [P, 1])
+        size = tile("size", [P, G])
+        under = tile("under", [P, G])
+        th = tile("th", [P, G])
+        ex = tile("ex", [P, G])
+        nc.scalar.activation(size[:], gap[:, 0:G], ACT.Abs, scale=st[:])
+        nc.scalar.activation(under[:], gap[:, 0:G], ACT.Relu, scale=st[:])
+        nc.scalar.activation(th[:], size[:], ACT.Tanh, scale=1.0 / 16.0)
+        nc.scalar.activation(ex[:], under[:], ACT.Exp, scale=-1.0 / 8.0)
+
+        nc.scalar.activation(st_m2[:], st[:], ACT.Copy, scale=-2.0)
+        nc.scalar.activation(st_m16[:], st[:], ACT.Copy, scale=-1.0 / 16.0)
+        go_bf = interleave("go_bf", go_raw)
+        val_words = gather("val_words", val_pool, U32, "block_sums")
+        go_mx = quantize("go", go_bf)
+        c = product("c", go_mx, val_words, val_scales)
+
+        gate2 = tile("gate2", [P, G], F32, "val_pool")
+        nc.vector.scalar_tensor_tensor(gate2[:], th[:], 1.0, ex[:], ALU.add, ALU.mult)
+        coef = tile("coef", [P, 2 * G])
+        nc.scalar.activation(coef[:, 0:G], gate2[:], ACT.Identity, scale=st[:], bias=st_m2[:])
+
+        p = tile("p", [P, I])
+        z = tile("z", [P, 1])
+        nc.vector.scalar_tensor_tensor(
+            by_group(p[:]), by_group(e[:]), 1.0, spread(gate2[:]), ALU.mult, ALU.mult, accum_out=z[:]
+        )
+        tau16 = tile("tau16", [P, G])
+        nc.vector.tensor_tensor(tau16[:], coef[:, 0:G], gap[:, G : 2 * G], ALU.mult)
+        r = tile("r", [P, 1])
+        nc.vector.reciprocal(r[:], z[:])
+        tt = tile("tt", [P, I])
+        nc.vector.scalar_tensor_tensor(
+            by_group(tt[:]), spread(tau16[:]), 1.0 / 16.0, by_group(ta[:]), ALU.mult, ALU.add
+        )
+
+        r_m512 = tile("r_m512", [P, 1])
+        p_m512 = tile("p_m512", [P, I])
+        nc.scalar.activation(r_m512[:], r[:], ACT.Copy, scale=-512.0)
+        nc.scalar.activation(p_m512[:], p[:], ACT.Copy, scale=r_m512[:])
+
+        pc_sum = tile("pc_sum", [P, 1])
+        pt_sum = tile("pt_sum", [P, 1])
+        c_mean = tile("c_mean", [P, 1])
+        t_mean = tile("t_mean", [P, 1])
+        y = tile("y", [P, I])
+        w = tile("w", [P, I])
+        nc.vector.scalar_tensor_tensor(y[:], c[:], 1.0, p[:], ALU.mult, ALU.mult, accum_out=pc_sum[:])
+        nc.scalar.activation(c_mean[:], pc_sum[:], ACT.Copy, scale=r[:])
+        nc.vector.scalar_tensor_tensor(w[:], tt[:], 1.0, p[:], ALU.mult, ALU.mult, accum_out=pt_sum[:])
+        nc.scalar.activation(t_mean[:], pt_sum[:], ACT.Copy, scale=r[:])
+        p_one = tile("p_one", [P, I])
+        nc.scalar.activation(p_one[:], p[:], ACT.Copy, scale=r[:])
+
+        w_sum = tile("w_sum", [P, 1])
+        x = tile("x", [P, I])
+        tail = tile("tail", [P, 2 * G])
+        half = I // 2
+        nc.vector.scalar_tensor_tensor(y[:], c[:], c_mean[:], p_m512[:], ALU.subtract, ALU.mult)
+        nc.vector.scalar_tensor_tensor(coef[:, G : 2 * G], tau16[:], st_m16[:], gate2[:], ALU.mult, ALU.mult)
+        nc.vector.scalar_tensor_tensor(w[:], tt[:], t_mean[:], y[:], ALU.subtract, ALU.mult, accum_out=w_sum[:])
+        nc.vector.tensor_reduce(tail[:, G : G + G // 2], by_group(y[:, 0:half]), AX.X, ALU.add)
+        nc.vector.scalar_tensor_tensor(x[:], p_one[:], w_sum[:], w[:], ALU.mult, ALU.subtract)
+        nc.vector.tensor_reduce(tail[:, G + G // 2 : 2 * G], by_group(y[:, half:I]), AX.X, ALU.add)
+        nc.vector.tensor_reduce(tail[:, 0:G], by_group(x[:]), AX.X, ALU.add)
+
+        terms = tile("terms", [P, 2 * G])
+        h = tile("h", [P, G])
+        h_block = tile("h_block", [P, B])
+        eps = tile("eps", [P, G])
+        eps_full = tile("eps_full", [P, I])
+        nc.vector.tensor_tensor(terms[:], coef[:], tail[:], ALU.mult)
+        nc.vector.tensor_reduce(h_block[:], terms[:].rearrange("p (k b j) -> p b k j", k=2, j=GROUP), AX.XY, ALU.add)
+        nc.vector.tensor_tensor(h[:], terms[:, 0:G], terms[:, G : 2 * G], ALU.add)
+        nc.vector.scalar_tensor_tensor(
+            by_group(eps[:]), spread(h_block[:]), -1.0 / 8.0, by_group(h[:]), ALU.mult, ALU.add
+        )
+        nc.vector.tensor_scalar(by_group(eps_full[:]), spread(eps[:]), -1.0 / 16.0, None, ALU.mult)
+
+        nc.vector.tensor_tensor(window[:].indirect(offsets[:]), x[:], eps_full[:], ALU.add)
+
+        lo = 0
+        for n, width in enumerate(OUT_CHUNKS):
+            cols = slice(lo, lo + width)
+            nc.vector.tensor_tensor(rest[:, cols], rest[:, cols], window[:, cols], ALU.add)
+            queue = nc.sync if n % 2 == 0 else nc.scalar
+            queue.dma_start(out[:, cols], rest[:, cols])
+            lo = lo + width

@@ -53,13 +53,13 @@ def tile_attend_hvblockcontrast_s_kernel(
                 )
             return plane
 
-        def load_words(name, src):
-            words = tile(name, [P, T], U32)
+        def load_words(name, src, tag=None):
+            words = tile(name, [P, T], U32, tag)
             nc.sync.dma_start(words[:].bitcast(I32), src[0].rearrange("p n t -> p (n t)").bitcast(I32))
             return words
 
-        def load_rows(name, src):
-            raw = tile(name, [P, PACK, Q])
+        def load_rows(name, src, tag=None):
+            raw = tile(name, [P, PACK, Q], F32, tag)
             nc.sync.dma_start(raw[:], src.rearrange("(p j) w -> p j w", j=PACK))
             return raw
 
@@ -70,8 +70,8 @@ def tile_attend_hvblockcontrast_s_kernel(
             )
             return grouped
 
-        def quantize(name, grouped):
-            codes = tile(name + "_codes", [P, Q], U32)
+        def quantize(name, grouped, tag=None):
+            codes = tile(name + "_codes", [P, Q], U32, tag)
             scales = tile(name + "_scales", [P, Q], U8)
             nc.vector.quantize_mx(
                 out=codes[:].bitcast(FP8X4), scales=scales[:], in_=grouped[:].rearrange("p w j -> p (w j)")
@@ -96,14 +96,18 @@ def tile_attend_hvblockcontrast_s_kernel(
             )
             return bank
 
+        st = tile("st", [P, 1])
+        nc.gpsimd.dma_start(st[:], steep)
+        st_8 = tile("st_8", [P, 1])
+        st_m16 = tile("st_m16", [P, 1])
+        nc.gpsimd.tensor_scalar(st_8[:], st[:], 1.0 / 8.0, None, ALU.mult)
+        nc.gpsimd.tensor_scalar(st_m16[:], st[:], -1.0 / 16.0, None, ALU.mult)
         q_raw = load_rows("q_raw", query)
         dq_raw = load_rows("dq_raw", dquery)
         key_plane = load_scales("key_plane", keys_scales, nc.vector)
         key_pool = load_words("key_pool", keys_words)
-        val_plane = load_scales("val_plane", vals_scales, nc.vector)
-        st = tile("st", [P, 1])
-        nc.sync.dma_start(st[:], steep)
         go_raw = load_rows("go_raw", gout)
+        val_plane = load_scales("val_plane", vals_scales, nc.vector)
         val_pool = load_words("val_pool", vals_words)
         rest = tile("rest", [P, T])
         nc.sync.dma_start(rest[:], base)
@@ -117,18 +121,19 @@ def tile_attend_hvblockcontrast_s_kernel(
         q_mx = quantize("q", q_bf)
         dq_mx = quantize("dq", dq_bf)
         key_words = gather("key_words", key_pool, U32)
-        val_scales = gather("val_scales", val_plane, U8, "q_bf")
+        go_bf = interleave("go_bf", go_raw)
+        val_scales = gather("val_scales", val_plane, U8)
         a = product("a", q_mx, key_words, key_scales)
         ta = product("ta", dq_mx, key_words, key_scales)
 
-        sums = tile("sums", [P, 2 * G])
-        nc.vector.tensor_reduce(sums[:, 0:G], by_group(a[:]), AX.X, ALU.add)
-
-        soft = tile("soft", [P, I])
+        soft = tile("soft", [P, I], F32, "go_raw")
         soft_sum = tile("soft_sum", [P, 1])
         shift = tile("shift", [P, 1])
         e = tile("e", [P, I])
+        sums = tile("sums", [P, 2 * G])
         nc.scalar.activation(soft[:], a[:], ACT.Exp, scale=1.0 / SOFT, accum_out=soft_sum[:])
+        nc.vector.tensor_reduce(sums[:, G : 2 * G], by_group(ta[:]), AX.X, ALU.add)
+        nc.vector.tensor_reduce(sums[:, 0:G], by_group(a[:]), AX.X, ALU.add)
         nc.scalar.activation(
             shift[:],
             soft_sum[:].bitcast(U32),
@@ -138,26 +143,13 @@ def tile_attend_hvblockcontrast_s_kernel(
         )
         nc.scalar.activation(e[:], a[:], ACT.Exp, bias=shift[:])
 
-        nc.vector.tensor_reduce(sums[:, G : 2 * G], by_group(ta[:]), AX.X, ALU.add)
         block_a = tile("block_sums", [P, B])
-        block_t = tile("block_t", [P, B])
         gap = tile("gap", [P, 2 * G])
         nc.vector.tensor_reduce(block_a[:], by_group(sums[:, 0:G]), AX.X, ALU.add)
         nc.vector.scalar_tensor_tensor(
             by_group(gap[:, 0:G]), spread(block_a[:]), 1.0 / 8.0, by_group(sums[:, 0:G]), ALU.mult, ALU.subtract
         )
-        nc.vector.tensor_reduce(block_t[:], by_group(sums[:, G : 2 * G]), AX.X, ALU.add)
-        nc.vector.scalar_tensor_tensor(
-            by_group(gap[:, G : 2 * G]),
-            spread(block_t[:]),
-            1.0 / 8.0,
-            by_group(sums[:, G : 2 * G]),
-            ALU.mult,
-            ALU.subtract,
-        )
 
-        st_m2 = tile("st_m2", [P, 1])
-        st_m16 = tile("st_m16", [P, 1])
         size = tile("size", [P, G])
         under = tile("under", [P, G])
         th = tile("th", [P, G])
@@ -167,81 +159,82 @@ def tile_attend_hvblockcontrast_s_kernel(
         nc.scalar.activation(th[:], size[:], ACT.Tanh, scale=1.0 / 16.0)
         nc.scalar.activation(ex[:], under[:], ACT.Exp, scale=-1.0 / 8.0)
 
-        nc.scalar.activation(st_m2[:], st[:], ACT.Copy, scale=-2.0)
-        nc.scalar.activation(st_m16[:], st[:], ACT.Copy, scale=-1.0 / 16.0)
-        go_bf = interleave("go_bf", go_raw)
         val_words = gather("val_words", val_pool, U32, "block_sums")
         go_mx = quantize("go", go_bf)
         c = product("c", go_mx, val_words, val_scales)
 
-        gate2 = tile("gate2", [P, G], F32, "val_pool")
-        nc.vector.scalar_tensor_tensor(gate2[:], th[:], 1.0, ex[:], ALU.add, ALU.mult)
-        coef = tile("coef", [P, 2 * G])
-        nc.scalar.activation(coef[:, 0:G], gate2[:], ACT.Identity, scale=st[:], bias=st_m2[:])
+        late = tile("late", [P, G + B], F32, "val_pool")
+        gate2 = late[:, 0:G]
+        block_t = late[:, G : G + B]
+        nc.vector.tensor_reduce(block_t, by_group(sums[:, G : 2 * G]), AX.X, ALU.add)
+        nc.vector.scalar_tensor_tensor(gate2, th[:], 1.0, ex[:], ALU.add, ALU.mult)
+        nc.vector.scalar_tensor_tensor(
+            by_group(gap[:, G : 2 * G]),
+            spread(block_t),
+            1.0 / 8.0,
+            by_group(sums[:, G : 2 * G]),
+            ALU.mult,
+            ALU.subtract,
+        )
+
+        coef = tile("coef", [P, 2, G])
+        nc.scalar.activation(coef[:, 0, :], gate2, ACT.Identity, scale=st_m16[:], bias=st_8[:])
 
         p = tile("p", [P, I])
         z = tile("z", [P, 1])
         nc.vector.scalar_tensor_tensor(
-            by_group(p[:]), by_group(e[:]), 1.0, spread(gate2[:]), ALU.mult, ALU.mult, accum_out=z[:]
+            by_group(p[:]), by_group(e[:]), 1.0, spread(gate2), ALU.mult, ALU.mult, accum_out=z[:]
         )
-        tau16 = tile("tau16", [P, G])
-        nc.vector.tensor_tensor(tau16[:], coef[:, 0:G], gap[:, G : 2 * G], ALU.mult)
+        tau = tile("tau", [P, G])
+        nc.vector.tensor_tensor(tau[:], coef[:, 0, :], gap[:, G : 2 * G], ALU.mult)
         r = tile("r", [P, 1])
         nc.vector.reciprocal(r[:], z[:])
         tt = tile("tt", [P, I])
-        nc.vector.scalar_tensor_tensor(
-            by_group(tt[:]), spread(tau16[:]), 1.0 / 16.0, by_group(ta[:]), ALU.mult, ALU.add
-        )
+        nc.vector.tensor_tensor(by_group(tt[:]), by_group(ta[:]), spread(tau[:]), ALU.subtract)
 
-        r_m512 = tile("r_m512", [P, 1])
-        p_m512 = tile("p_m512", [P, I])
-        nc.scalar.activation(r_m512[:], r[:], ACT.Copy, scale=-512.0)
-        nc.scalar.activation(p_m512[:], p[:], ACT.Copy, scale=r_m512[:])
-
-        pc_sum = tile("pc_sum", [P, 1])
-        pt_sum = tile("pt_sum", [P, 1])
         c_mean = tile("c_mean", [P, 1])
         t_mean = tile("t_mean", [P, 1])
         y = tile("y", [P, I])
         w = tile("w", [P, I])
-        nc.vector.scalar_tensor_tensor(y[:], c[:], 1.0, p[:], ALU.mult, ALU.mult, accum_out=pc_sum[:])
-        nc.scalar.activation(c_mean[:], pc_sum[:], ACT.Copy, scale=r[:])
-        nc.vector.scalar_tensor_tensor(w[:], tt[:], 1.0, p[:], ALU.mult, ALU.mult, accum_out=pt_sum[:])
-        nc.scalar.activation(t_mean[:], pt_sum[:], ACT.Copy, scale=r[:])
-        p_one = tile("p_one", [P, I])
+        nc.vector.scalar_tensor_tensor(y[:], c[:], r[:], p[:], ALU.mult, ALU.mult, accum_out=c_mean[:])
+        nc.vector.scalar_tensor_tensor(w[:], tt[:], r[:], p[:], ALU.mult, ALU.mult, accum_out=t_mean[:])
+        p_one = tile("p_one", [P, I], F32, "e")
+        r_m512 = tile("r_m512", [P, 1])
         nc.scalar.activation(p_one[:], p[:], ACT.Copy, scale=r[:])
+        nc.scalar.activation(r_m512[:], r[:], ACT.Copy, scale=-512.0)
 
         w_sum = tile("w_sum", [P, 1])
         x = tile("x", [P, I])
-        tail = tile("tail", [P, 2 * G])
+        tail = tile("tail", [P, 2, G])
         half = I // 2
-        nc.vector.scalar_tensor_tensor(y[:], c[:], c_mean[:], p_m512[:], ALU.subtract, ALU.mult)
-        nc.vector.scalar_tensor_tensor(coef[:, G : 2 * G], tau16[:], st_m16[:], gate2[:], ALU.mult, ALU.mult)
+        nc.vector.scalar_tensor_tensor(y[:], c[:], c_mean[:], p[:], ALU.subtract, ALU.mult)
+        nc.vector.scalar_tensor_tensor(coef[:, 1, :], tau[:], st_m16[:], gate2, ALU.mult, ALU.mult)
         nc.vector.scalar_tensor_tensor(w[:], tt[:], t_mean[:], y[:], ALU.subtract, ALU.mult, accum_out=w_sum[:])
-        nc.vector.tensor_reduce(tail[:, G : G + G // 2], by_group(y[:, 0:half]), AX.X, ALU.add)
+        nc.vector.tensor_reduce(tail[:, 1, 0 : G // 2], by_group(y[:, 0:half]), AX.X, ALU.add)
         nc.vector.scalar_tensor_tensor(x[:], p_one[:], w_sum[:], w[:], ALU.mult, ALU.subtract)
-        nc.vector.tensor_reduce(tail[:, G + G // 2 : 2 * G], by_group(y[:, half:I]), AX.X, ALU.add)
-        nc.vector.tensor_reduce(tail[:, 0:G], by_group(x[:]), AX.X, ALU.add)
+        nc.vector.tensor_reduce(tail[:, 1, G // 2 : G], by_group(y[:, half:I]), AX.X, ALU.add)
+        nc.vector.tensor_reduce(tail[:, 0, :], by_group(x[:]), AX.X, ALU.add)
 
-        terms = tile("terms", [P, 2 * G])
+        terms = tile("terms", [P, 2, G])
         h = tile("h", [P, G])
         h_block = tile("h_block", [P, B])
-        eps = tile("eps", [P, G])
         eps_full = tile("eps_full", [P, I])
         nc.vector.tensor_tensor(terms[:], coef[:], tail[:], ALU.mult)
-        nc.vector.tensor_reduce(h_block[:], terms[:].rearrange("p (k b j) -> p b k j", k=2, j=GROUP), AX.XY, ALU.add)
-        nc.vector.tensor_tensor(h[:], terms[:, 0:G], terms[:, G : 2 * G], ALU.add)
+        nc.vector.tensor_reduce(h_block[:], terms[:].rearrange("p k (b j) -> p b k j", j=GROUP), AX.XY, ALU.add)
+        nc.vector.tensor_tensor(h[:], terms[:, 0, :], terms[:, 1, :], ALU.add)
+        eps = tile("eps", [P, G])
         nc.vector.scalar_tensor_tensor(
             by_group(eps[:]), spread(h_block[:]), -1.0 / 8.0, by_group(h[:]), ALU.mult, ALU.add
         )
-        nc.vector.tensor_scalar(by_group(eps_full[:]), spread(eps[:]), -1.0 / 16.0, None, ALU.mult)
-
+        nc.vector.tensor_copy(by_group(eps_full[:]), spread(eps[:]))
         nc.vector.tensor_tensor(window[:].indirect(offsets[:]), x[:], eps_full[:], ALU.add)
 
         lo = 0
         for n, width in enumerate(OUT_CHUNKS):
             cols = slice(lo, lo + width)
-            nc.vector.tensor_tensor(rest[:, cols], rest[:, cols], window[:, cols], ALU.add)
+            nc.vector.scalar_tensor_tensor(
+                rest[:, cols], window[:, cols], r_m512[:], rest[:, cols], ALU.mult, ALU.add
+            )
             queue = nc.sync if n % 2 == 0 else nc.scalar
             queue.dma_start(out[:, cols], rest[:, cols])
             lo = lo + width

@@ -126,14 +126,25 @@ def tile_attend_hvblockcontrast_s_kernel(
         a = product("a", q_mx, key_words, key_scales)
         ta = product("ta", dq_mx, key_words, key_scales)
 
+        sums = tile("sums", [P, 2 * G], F32, "val_plane")
+        nc.vector.tensor_reduce(sums[:, 0:G], by_group(a[:]), AX.X, ALU.add)
+        nc.vector.tensor_reduce(sums[:, G : 2 * G], by_group(ta[:]), AX.X, ALU.add)
+        block_a = tile("block_sums", [P, B])
+        gap_a = tile("gap_a", [P, G])
+        gap_t = tile("gap_t", [P, G])
+        nc.vector.tensor_reduce(block_a[:], by_group(sums[:, 0:G]), AX.X, ALU.add)
+        nc.vector.scalar_tensor_tensor(
+            by_group(gap_a[:]), spread(block_a[:]), 1.0 / 8.0, by_group(sums[:, 0:G]), ALU.mult, ALU.subtract
+        )
+
         soft = tile("soft", [P, I], F32, "go_raw")
         soft_sum = tile("soft_sum", [P, 1])
         shift = tile("shift", [P, 1])
-        e = tile("e", [P, I])
-        sums = tile("sums", [P, 2 * G])
+        size = tile("size", [P, G])
+        under = tile("under", [P, G])
+        th = tile("th", [P, G])
+        ex = tile("ex", [P, G])
         nc.scalar.activation(soft[:], a[:], ACT.Exp, scale=1.0 / SOFT, accum_out=soft_sum[:])
-        nc.vector.tensor_reduce(sums[:, G : 2 * G], by_group(ta[:]), AX.X, ALU.add)
-        nc.vector.tensor_reduce(sums[:, 0:G], by_group(a[:]), AX.X, ALU.add)
         nc.scalar.activation(
             shift[:],
             soft_sum[:].bitcast(U32),
@@ -141,26 +152,15 @@ def tile_attend_hvblockcontrast_s_kernel(
             scale=-SOFT * math.log(2.0) / 2.0**23,
             bias=SOFT * (127.0 * math.log(2.0) + math.log(I)),
         )
+        e = tile("e", [P, I])
         nc.scalar.activation(e[:], a[:], ACT.Exp, bias=shift[:])
-
-        block_a = tile("block_sums", [P, B])
-        gap = tile("gap", [P, 2 * G])
-        nc.vector.tensor_reduce(block_a[:], by_group(sums[:, 0:G]), AX.X, ALU.add)
-        nc.vector.scalar_tensor_tensor(
-            by_group(gap[:, 0:G]), spread(block_a[:]), 1.0 / 8.0, by_group(sums[:, 0:G]), ALU.mult, ALU.subtract
-        )
-
-        size = tile("size", [P, G])
-        under = tile("under", [P, G])
-        th = tile("th", [P, G])
-        ex = tile("ex", [P, G])
-        nc.scalar.activation(size[:], gap[:, 0:G], ACT.Abs, scale=st[:])
-        nc.scalar.activation(under[:], gap[:, 0:G], ACT.Relu, scale=st[:])
+        nc.scalar.activation(size[:], gap_a[:], ACT.Abs, scale=st[:])
+        nc.scalar.activation(under[:], gap_a[:], ACT.Relu, scale=st[:])
         nc.scalar.activation(th[:], size[:], ACT.Tanh, scale=1.0 / 16.0)
         nc.scalar.activation(ex[:], under[:], ACT.Exp, scale=-1.0 / 8.0)
 
-        val_words = gather("val_words", val_pool, U32, "block_sums")
         go_mx = quantize("go", go_bf)
+        val_words = gather("val_words", val_pool, U32, "block_sums")
         c = product("c", go_mx, val_words, val_scales)
 
         late = tile("late", [P, G + B], F32, "val_pool")
@@ -169,7 +169,7 @@ def tile_attend_hvblockcontrast_s_kernel(
         nc.vector.tensor_reduce(block_t, by_group(sums[:, G : 2 * G]), AX.X, ALU.add)
         nc.vector.scalar_tensor_tensor(gate2, th[:], 1.0, ex[:], ALU.add, ALU.mult)
         nc.vector.scalar_tensor_tensor(
-            by_group(gap[:, G : 2 * G]),
+            by_group(gap_t[:]),
             spread(block_t),
             1.0 / 8.0,
             by_group(sums[:, G : 2 * G]),
@@ -186,7 +186,7 @@ def tile_attend_hvblockcontrast_s_kernel(
             by_group(p[:]), by_group(e[:]), 1.0, spread(gate2), ALU.mult, ALU.mult, accum_out=z[:]
         )
         tau = tile("tau", [P, G])
-        nc.vector.tensor_tensor(tau[:], coef[:, 0, :], gap[:, G : 2 * G], ALU.mult)
+        nc.vector.tensor_tensor(tau[:], coef[:, 0, :], gap_t[:], ALU.mult)
         r = tile("r", [P, 1])
         nc.vector.reciprocal(r[:], z[:])
         tt = tile("tt", [P, I])
@@ -198,7 +198,7 @@ def tile_attend_hvblockcontrast_s_kernel(
         w = tile("w", [P, I])
         nc.vector.scalar_tensor_tensor(y[:], c[:], r[:], p[:], ALU.mult, ALU.mult, accum_out=c_mean[:])
         nc.vector.scalar_tensor_tensor(w[:], tt[:], r[:], p[:], ALU.mult, ALU.mult, accum_out=t_mean[:])
-        p_one = tile("p_one", [P, I], F32, "e")
+        p_one = tile("p_one", [P, I])
         r_m512 = tile("r_m512", [P, 1])
         nc.scalar.activation(p_one[:], p[:], ACT.Copy, scale=r[:])
         nc.scalar.activation(r_m512[:], r[:], ACT.Copy, scale=-512.0)

@@ -113,7 +113,7 @@ def tile_attend_hvblockcontrast_s_kernel(
         nc.sync.dma_start(rest[:], base)
 
         window = tile("window", [P, T])
-        nc.vector.memset(window[:], 0.0)
+        nc.gpsimd.memset(window[:], 0.0)
 
         key_scales = gather("key_scales", key_plane, U8)
         q_bf = interleave("q_bf", q_raw)

import math
from contextlib import ExitStack

import concourse.mybir as mybir

D, T, I, Q, G, B = 512, 2048, 512, 128, 64, 8
GROUP = I // G
FLOPS = 3 * 2 * D * Q * I

F32 = mybir.dt.float32
BF16 = mybir.dt.bfloat16
I32 = mybir.dt.int32
U32 = mybir.dt.uint32
U16 = mybir.dt.uint16
U8 = mybir.dt.uint8
FP8X4 = mybir.dt.float8_e4m3fn_x4
ALU = mybir.AluOpType
ACT = mybir.ActivationFunctionType
AX = mybir.AxisListType

P = 128
PACK = 4
SOFT = 8.0
OUT_CHUNKS = [256, 512, 512, 512, 256]


def tile_attend_hvblockcontrast_s_kernel(
    tc, query, keys_words, keys_scales, steep, gout, vals_words, vals_scales, dquery, base, offs, out
):
    nc = tc.nc
    with ExitStack() as ctx:
        keep = ctx.enter_context(tc.tile_pool(name="keep", bufs=1))
        psum = ctx.enter_context(tc.psum_pool(name="psum", bufs=1))

        def tile(name, shape, dtype=F32, tag=None):
            return keep.tile(shape, dtype, name=name, tag=tag or name, align_bytes=64)

        def by_group(ap):
            return ap.rearrange("p (g j) -> p g j", j=GROUP)

        def spread(ap):
            return ap.unsqueeze(2).to_broadcast([P, ap.shape[1], GROUP])

        offsets = keep.tile([P, I // 16], U16, name="offsets")
        nc.sync.dma_start(offsets[:], offs)

        def load_scales(name, src, engine):
            plane = tile(name, [P, T], U8)
            engine.memset(plane[:].bitcast(I32), 0)
            for quad in range(4):
                nc.sync.dma_start(
                    plane[32 * quad : 32 * quad + 4, :].bitcast(I32), src[0, 4 * quad : 4 * quad + 4, :].bitcast(I32)
                )
            return plane

        def load_words(name, src, tag=None):
            words = tile(name, [P, T], U32, tag)
            nc.sync.dma_start(words[:].bitcast(I32), src[0].rearrange("p n t -> p (n t)").bitcast(I32))
            return words

        def load_rows(name, src, tag=None):
            raw = tile(name, [P, PACK, Q], F32, tag)
            nc.sync.dma_start(raw[:], src.rearrange("(p j) w -> p j w", j=PACK))
            return raw

        def interleave(name, raw):
            grouped = tile(name, [P, Q, PACK], BF16)
            nc.scalar.copy(
                grouped[:].rearrange("p (c i) t -> p c t i", i=4), raw[:].rearrange("p t (c i) -> p c t i", i=4)
            )
            return grouped

        def quantize(name, grouped, tag=None):
            codes = tile(name + "_codes", [P, Q], U32, tag)
            scales = tile(name + "_scales", [P, Q], U8)
            nc.vector.quantize_mx(
                out=codes[:].bitcast(FP8X4), scales=scales[:], in_=grouped[:].rearrange("p w j -> p (w j)")
            )
            return codes, scales

        def gather(name, window, dtype, tag=None):
            picked = tile(name, [P, I], dtype, tag)
            nc.vector.tensor_copy(picked[:], window[:].indirect(offsets[:]))
            return picked

        def product(name, rows, words, scales):
            bank = psum.tile([P, I], F32, name=name)
            nc.tensor.matmul_mx(
                out=bank[:],
                lhsT=rows[0][:].bitcast(FP8X4),
                lhsT_scale=rows[1][:],
                rhs=words[:].bitcast(FP8X4),
                rhs_scale=scales[:],
                start=True,
                stop=True,
            )
            return bank

        st = tile("st", [P, 1])
        nc.gpsimd.dma_start(st[:], steep)
        st_8 = tile("st_8", [P, 1])
        st_m16 = tile("st_m16", [P, 1])
        nc.gpsimd.tensor_scalar(st_8[:], st[:], 1.0 / 8.0, None, ALU.mult)
        nc.gpsimd.tensor_scalar(st_m16[:], st[:], -1.0 / 16.0, None, ALU.mult)
        q_raw = load_rows("q_raw", query)
        dq_raw = load_rows("dq_raw", dquery)
        key_plane = load_scales("key_plane", keys_scales, nc.vector)
        key_pool = load_words("key_pool", keys_words)
        go_raw = load_rows("go_raw", gout)
        val_plane = load_scales("val_plane", vals_scales, nc.vector)
        val_pool = load_words("val_pool", vals_words)
        rest = tile("rest", [P, T])
        nc.sync.dma_start(rest[:], base)

        window = tile("window", [P, T])
        nc.gpsimd.memset(window[:], 0.0)

        key_scales = gather("key_scales", key_plane, U8)
        q_bf = interleave("q_bf", q_raw)
        dq_bf = interleave("dq_bf", dq_raw)
        q_mx = quantize("q", q_bf)
        dq_mx = quantize("dq", dq_bf)
        key_words = gather("key_words", key_pool, U32)
        go_bf = interleave("go_bf", go_raw)
        val_scales = gather("val_scales", val_plane, U8)
        a = product("a", q_mx, key_words, key_scales)
        ta = product("ta", dq_mx, key_words, key_scales)

        sums = tile("sums", [P, 2 * G], F32, "val_plane")
        nc.vector.tensor_reduce(sums[:, 0:G], by_group(a[:]), AX.X, ALU.add)
        nc.vector.tensor_reduce(sums[:, G : 2 * G], by_group(ta[:]), AX.X, ALU.add)
        block_a = tile("block_sums", [P, B])
        gap_a = tile("gap_a", [P, G])
        gap_t = tile("gap_t", [P, G])
        nc.vector.tensor_reduce(block_a[:], by_group(sums[:, 0:G]), AX.X, ALU.add)
        nc.vector.scalar_tensor_tensor(
            by_group(gap_a[:]), spread(block_a[:]), 1.0 / 8.0, by_group(sums[:, 0:G]), ALU.mult, ALU.subtract
        )

        soft = tile("soft", [P, I], F32, "go_raw")
        soft_sum = tile("soft_sum", [P, 1])
        shift = tile("shift", [P, 1])
        size = tile("size", [P, G])
        under = tile("under", [P, G])
        th = tile("th", [P, G])
        ex = tile("ex", [P, G])
        nc.scalar.activation(soft[:], a[:], ACT.Exp, scale=1.0 / SOFT, accum_out=soft_sum[:])
        nc.scalar.activation(
            shift[:],
            soft_sum[:].bitcast(U32),
            ACT.Copy,
            scale=-SOFT * math.log(2.0) / 2.0**23,
            bias=SOFT * (127.0 * math.log(2.0) + math.log(I)),
        )
        e = tile("e", [P, I])
        nc.scalar.activation(e[:], a[:], ACT.Exp, bias=shift[:])
        nc.scalar.activation(size[:], gap_a[:], ACT.Abs, scale=st[:])
        nc.scalar.activation(under[:], gap_a[:], ACT.Relu, scale=st[:])
        nc.scalar.activation(th[:], size[:], ACT.Tanh, scale=1.0 / 16.0)
        nc.scalar.activation(ex[:], under[:], ACT.Exp, scale=-1.0 / 8.0)

        go_mx = quantize("go", go_bf)
        val_words = gather("val_words", val_pool, U32, "block_sums")
        c = product("c", go_mx, val_words, val_scales)

        late = tile("late", [P, G + B], F32, "val_pool")
        gate2 = late[:, 0:G]
        block_t = late[:, G : G + B]
        nc.vector.tensor_reduce(block_t, by_group(sums[:, G : 2 * G]), AX.X, ALU.add)
        nc.vector.scalar_tensor_tensor(gate2, th[:], 1.0, ex[:], ALU.add, ALU.mult)
        nc.vector.scalar_tensor_tensor(
            by_group(gap_t[:]),
            spread(block_t),
            1.0 / 8.0,
            by_group(sums[:, G : 2 * G]),
            ALU.mult,
            ALU.subtract,
        )

        coef = tile("coef", [P, 2, G])
        nc.scalar.activation(coef[:, 0, :], gate2, ACT.Identity, scale=st_m16[:], bias=st_8[:])

        p = tile("p", [P, I])
        z = tile("z", [P, 1])
        nc.vector.scalar_tensor_tensor(
            by_group(p[:]), by_group(e[:]), 1.0, spread(gate2), ALU.mult, ALU.mult, accum_out=z[:]
        )
        tau = tile("tau", [P, G])
        nc.vector.tensor_tensor(tau[:], coef[:, 0, :], gap_t[:], ALU.mult)
        r = tile("r", [P, 1])
        nc.vector.reciprocal(r[:], z[:])
        tt = tile("tt", [P, I])
        nc.vector.tensor_tensor(by_group(tt[:]), by_group(ta[:]), spread(tau[:]), ALU.subtract)

        c_mean = tile("c_mean", [P, 1])
        t_mean = tile("t_mean", [P, 1])
        y = tile("y", [P, I])
        w = tile("w", [P, I])
        nc.vector.scalar_tensor_tensor(y[:], c[:], r[:], p[:], ALU.mult, ALU.mult, accum_out=c_mean[:])
        nc.vector.scalar_tensor_tensor(w[:], tt[:], r[:], p[:], ALU.mult, ALU.mult, accum_out=t_mean[:])
        p_one = tile("p_one", [P, I])
        r_m512 = tile("r_m512", [P, 1])
        nc.scalar.activation(p_one[:], p[:], ACT.Copy, scale=r[:])
        nc.scalar.activation(r_m512[:], r[:], ACT.Copy, scale=-512.0)

        w_sum = tile("w_sum", [P, 1])
        x = tile("x", [P, I])
        tail = tile("tail", [P, 2, G])
        half = I // 2
        nc.vector.scalar_tensor_tensor(y[:], c[:], c_mean[:], p[:], ALU.subtract, ALU.mult)
        nc.vector.scalar_tensor_tensor(coef[:, 1, :], tau[:], st_m16[:], gate2, ALU.mult, ALU.mult)
        nc.vector.scalar_tensor_tensor(w[:], tt[:], t_mean[:], y[:], ALU.subtract, ALU.mult, accum_out=w_sum[:])
        nc.vector.tensor_reduce(tail[:, 1, 0 : G // 2], by_group(y[:, 0:half]), AX.X, ALU.add)
        nc.vector.scalar_tensor_tensor(x[:], p_one[:], w_sum[:], w[:], ALU.mult, ALU.subtract)
        nc.vector.tensor_reduce(tail[:, 1, G // 2 : G], by_group(y[:, half:I]), AX.X, ALU.add)
        nc.vector.tensor_reduce(tail[:, 0, :], by_group(x[:]), AX.X, ALU.add)

        terms = tile("terms", [P, 2, G])
        h = tile("h", [P, G])
        h_block = tile("h_block", [P, B])
        eps_full = tile("eps_full", [P, I])
        nc.vector.tensor_tensor(terms[:], coef[:], tail[:], ALU.mult)
        nc.vector.tensor_reduce(h_block[:], terms[:].rearrange("p k (b j) -> p b k j", j=GROUP), AX.XY, ALU.add)
        nc.vector.tensor_tensor(h[:], terms[:, 0, :], terms[:, 1, :], ALU.add)
        eps = tile("eps", [P, G])
        nc.vector.scalar_tensor_tensor(
            by_group(eps[:]), spread(h_block[:]), -1.0 / 8.0, by_group(h[:]), ALU.mult, ALU.add
        )
        nc.vector.tensor_copy(by_group(eps_full[:]), spread(eps[:]))
        nc.vector.tensor_tensor(window[:].indirect(offsets[:]), x[:], eps_full[:], ALU.add)

        lo = 0
        for n, width in enumerate(OUT_CHUNKS):
            cols = slice(lo, lo + width)
            nc.vector.scalar_tensor_tensor(
                rest[:, cols], window[:, cols], r_m512[:], rest[:, cols], ALU.mult, ALU.add
            )
            queue = nc.sync if n % 2 == 0 else nc.scalar
            queue.dma_start(out[:, cols], rest[:, cols])
            lo = lo + width
